import numpy as np
import ml_dtypes


def mxq(x, axis, fmt="e4m3"):
    dtype, down = {"e4m3": (ml_dtypes.float8_e4m3fn, 7), "e5m2": (ml_dtypes.float8_e5m2, 14)}[fmt]
    v = np.moveaxis(np.asarray(x, np.float32).astype(ml_dtypes.bfloat16).astype(np.float64), axis, -1)
    blocks = v.reshape(v.shape[:-1] + (-1, 32))
    amax = np.abs(blocks).max(-1, keepdims=True)
    byte = np.maximum(np.where(amax > 0, np.frexp(amax)[1] - 1 + 127, 0) - down, 1)
    scale = np.exp2(byte - 127.0)
    codes = (blocks / scale).astype(np.float32).astype(dtype).astype(np.float64)
    return np.moveaxis((codes * scale).reshape(v.shape), -1, axis)


WIDE = False


def mx_kscale(k):
    if not WIDE:
        return np.ones(k)
    levels = np.array([10, -10, 5, -5, 0])
    if k % 512:
        return np.exp2(np.random.permutation(np.resize(levels, k // 32))).repeat(32)
    a = np.empty((k // 512, 16))
    for p in range(k // 512):
        a[p, :8] = np.random.permutation(np.resize(levels, 8))
        for g in range(8):
            far = levels[np.abs(levels - a[p, g]) >= 10]
            a[p, g + 8] = far[np.random.randint(len(far))]
    return np.exp2(a.ravel()).repeat(32)


def f64(x):
    return np.asarray(x).astype(np.float64)


def striped(idx):
    return np.tile(idx.reshape(-1, 16).T, (8, 1)).astype(np.uint16)


def unstriped(offs):
    return offs[:16].T.reshape(-1).astype(np.int64)


def striped8(idx):
    return np.concatenate([x.reshape(-1, 16).T for x in idx]).astype(np.uint16)


def runs(offs, k):
    lists = np.stack([offs[16 * r : 16 * r + 16].T.reshape(-1) for r in range(8)]).astype(np.int64)
    return lists[np.arange(k) % 512 // 64]


def pack_weight(w):
    k, n = w.shape
    w = f64(np.asarray(w, np.float32).astype(ml_dtypes.bfloat16)).reshape(k // 32, 32, n)
    amax = np.abs(w).max(1)
    byte = np.clip(np.where(amax > 0, np.frexp(amax)[1] - 1 + 127 - 7, 1), 1, 254)
    scaled = (w * np.exp2(127.0 - byte)[:, None, :]).reshape(k, n).astype(np.float32)
    words = np.ascontiguousarray(scaled.reshape(k // 512, 128, 4, n).transpose(0, 1, 3, 2)).astype(ml_dtypes.float8_e4m3fn).view(np.uint8)
    return words, np.ascontiguousarray(byte.astype(np.uint8).reshape(k // 512, 16, n))


def unpack_weight(words, scales):
    g, p, n, _ = words.shape
    vals = np.ascontiguousarray(words).view(ml_dtypes.float8_e4m3fn).astype(np.float64) * np.repeat(np.exp2(scales.astype(np.float64) - 127.0), 8, axis=1)[..., None]
    return vals.transpose(0, 1, 3, 2).reshape(g * 512, n)


E2M1 = np.array([0.0, 0.5, 1.0, 1.5, 2.0, 3.0, 4.0, 6.0, -0.0, -0.5, -1.0, -1.5, -2.0, -3.0, -4.0, -6.0])


def pack_fp4(w):
    k, n = w.shape
    w = f64(np.asarray(w, np.float32).astype(ml_dtypes.bfloat16)).reshape(k // 32, 32, n)
    amax = np.abs(w).max(1)
    mant, ex = np.frexp(amax / 6.0)
    byte = np.clip(np.where(amax > 0, np.where(mant > 0.5, ex, ex - 1) + 127, 1), 1, 254)
    scaled = (w * np.exp2(127.0 - byte)[:, None, :]).reshape(k, n).astype(np.float32)
    c = np.ascontiguousarray(scaled.reshape(k // 512, 128, 4, n).transpose(0, 1, 3, 2)).astype(ml_dtypes.float4_e2m1fn).view(np.uint8) & 0xF
    words = (c[..., 0::2] | (c[..., 1::2] << 4)).reshape(k // 512, 128, 2 * n)
    return np.ascontiguousarray(words), np.ascontiguousarray(byte.astype(np.uint8).reshape(k // 512, 16, n))


def unpack_fp4(words, scales):
    g, _, n = scales.shape
    words = np.ascontiguousarray(words).reshape(g, 128, n, 2)
    nib = np.empty((g, 128, n, 4), np.uint8)
    nib[..., 0::2] = words & 0xF
    nib[..., 1::2] = words >> 4
    vals = E2M1[nib] * np.repeat(np.exp2(scales.astype(np.float64) - 127.0), 8, axis=1)[..., None]
    return vals.transpose(0, 1, 3, 2).reshape(g * 512, n)


def relu(v):
    return np.maximum(v, 0.0)


def sigmoid(v):
    return 1.0 / (1.0 + np.exp(-np.maximum(v, -700.0)))


K, T, S, N, G, H = 512, 2048, 256, 512, 2048, 512


def setup_inputs():
    n = np.random.standard_normal
    s = mx_kscale(K)[:, None]
    u = mx_kscale(K)
    packed_xT = pack_weight(n((K, T)) * s)
    packed_dT = pack_weight(n((K, G)) / s)
    packed_w1 = pack_fp4(n((H, N)) / np.sqrt(H) / u[:, None])
    return {
        "x_words": packed_xT[0],
        "x_scales": packed_xT[1],
        "d_words": packed_dT[0],
        "d_scales": packed_dT[1],
        "sl": np.random.uniform(1.0, 2.0, (H, 1)).astype(np.float32),
        "th": (0.5 * n((H, 1))).astype(np.float32),
        "gn": (np.random.uniform(0.5, 1.5, (H, 1)) * u[:, None]).astype(np.float32),
        "w1_words": packed_w1[0],
        "w1_scales": packed_w1[1],
        "offs": striped(np.random.permutation(T)[:S]),
        "ci": striped(np.random.permutation(G)[:H]),
        "n1": striped8(np.stack([np.random.permutation(S) for _ in range(8)])),
        "n2": striped8(np.stack([np.random.permutation(S) for _ in range(8)])),
        "n3": striped(np.random.permutation(S)),
    }


def reference(x_words, x_scales, d_words, d_scales, sl, th, gn, w1_words, w1_scales, offs, ci, n1, n2, n3):
    d_ci = unpack_weight(d_words, d_scales)[:, unstriped(ci)]
    xq = unpack_weight(x_words, x_scales)[:, unstriped(offs)]
    s = 0.0625 * (d_ci.T @ xq)
    st = np.maximum(s, s[np.arange(H)[:, None], runs(n1, H)])
    sg = sigmoid(f64(sl) * (st[np.arange(H)[:, None], runs(n2, H)] - f64(th)))
    z = f64(gn) * (st * sg)
    h = unpack_fp4(w1_words, w1_scales).T @ mxq(z, 0, "e4m3")
    rl = relu(h)
    ds = np.zeros((N, S))
    ds[:, unstriped(n3)] = rl
    return ds - (0.5 * h)

@@ -1,0 +1,162 @@
+from contextlib import ExitStack
+
+import concourse.mybir as mybir
+
+F32 = mybir.dt.float32
+BF16 = mybir.dt.bfloat16
+I32 = mybir.dt.int32
+U32 = mybir.dt.uint32
+U16 = mybir.dt.uint16
+U8 = mybir.dt.uint8
+FP8X4 = mybir.dt.float8_e4m3fn_x4
+FP4X4 = mybir.dt.float4_e2m1fn_x4
+ALU = mybir.AluOpType
+ACT = mybir.ActivationFunctionType
+
+P = 128
+PACK = 4
+TABLE = 2048
+S = 256
+H = 512
+N = 512
+HALF = S // 2
+LIST_ROWS = 16
+SCORE_SCALE = 0.0625
+
+FLOPS = 2 * 512 * H * S + 2 * H * N * S
+
+
+def load_scale_rows(queues, plane, scales):
+    for q, queue in enumerate(queues):
+        queue.dma_start(out=plane[32 * q : 32 * q + 4, :].bitcast(I32), in_=scales[0, 4 * q : 4 * q + 4, :].bitcast(I32))
+
+
+def tile_picked_dwlehhsend_none_p_kernel(tc, x_words, x_scales, d_words, d_scales, sl, th, gn, w1_words, w1_scales, offs, ci, n1, n2, n3, out):
+    nc = tc.nc
+    with ExitStack() as ctx:
+        keep = ctx.enter_context(tc.tile_pool(name="keep", bufs=1))
+        psum = ctx.enter_context(tc.psum_pool(name="psum", bufs=1))
+
+        def half_of(list_tile, a):
+            cols = HALF // LIST_ROWS
+            return list_tile[:, a * cols : (a + 1) * cols]
+
+        ci_list = keep.tile([P, H // LIST_ROWS], U16, name="ci_list")
+        offs_list = keep.tile([P, S // LIST_ROWS], U16, name="offs_list")
+        n1_list = keep.tile([P, S // LIST_ROWS], U16, name="n1_list")
+        n2_list = keep.tile([P, S // LIST_ROWS], U16, name="n2_list")
+        n3_list = keep.tile([P, S // LIST_ROWS], U16, name="n3_list")
+
+        d_table = keep.tile([P, TABLE], U32, name="d_table")
+        x_table = keep.tile([P, TABLE], U32, name="x_table")
+        d_table_scales = keep.tile([P, TABLE], U8, name="d_table_scales")
+        x_table_scales = keep.tile([P, TABLE], U8, name="x_table_scales")
+        w1_codes = keep.tile([P, 2 * N], U8, name="w1_codes", align_bytes=64)
+        w1_plane = keep.tile([P, N], U8, name="w1_plane", align_bytes=64)
+        slope = keep.tile([P, PACK], F32, name="slope")
+        threshold = keep.tile([P, PACK], F32, name="threshold")
+        gain = keep.tile([P, PACK], F32, name="gain")
+        bias = keep.tile([P, PACK], F32, name="bias")
+
+        nc.vector.memset(d_table_scales[:].bitcast(I32), 0)
+        nc.vector.memset(x_table_scales[:].bitcast(I32), 0)
+        nc.vector.memset(w1_plane[:].bitcast(I32), 0)
+
+        s_rows = [keep.tile([P, 2 * S], F32, name=f"s_row{t}") for t in range(PACK)]
+        for s_row in s_rows:
+            nc.vector.memset(s_row[:, S:], 0.0)
+
+        nc.sync.dma_start(ci_list[:], ci)
+        nc.sync.dma_start(offs_list[:], offs)
+        nc.sync.dma_start(out=d_table[:].bitcast(I32), in_=d_words[0].rearrange("p n t -> p (n t)").bitcast(I32))
+        load_scale_rows([nc.scalar] * 4, d_table_scales, d_scales)
+        nc.sync.dma_start(out=x_table[:].bitcast(I32), in_=x_words[0].rearrange("p n t -> p (n t)").bitcast(I32))
+        load_scale_rows([nc.scalar] * 3 + [nc.gpsimd], x_table_scales, x_scales)
+        load_scale_rows([nc.scalar] * 4, w1_plane, w1_scales)
+        nc.sync.dma_start(n1_list[:], n1)
+        nc.sync.dma_start(n2_list[:], n2)
+        nc.sync.dma_start(out=slope[:], in_=sl.rearrange("(p t) o -> p (t o)", t=PACK))
+        nc.sync.dma_start(out=threshold[:], in_=th.rearrange("(p t) o -> p (t o)", t=PACK))
+        nc.sync.dma_start(out=gain[:], in_=gn.rearrange("(p t) o -> p (t o)", t=PACK))
+        nc.sync.dma_start(out=w1_codes[:].bitcast(I32), in_=w1_words[0].bitcast(I32))
+        nc.sync.dma_start(n3_list[:], n3)
+
+        d_codes = keep.tile([P, PACK, P], U32, name="d_codes", align_bytes=64)
+        d_plane = keep.tile([P, PACK, P], U8, name="d_plane", align_bytes=64)
+        x_codes = keep.tile([P, S], U32, name="x_codes", align_bytes=64)
+        x_plane = keep.tile([P, S], U8, name="x_plane", align_bytes=64)
+        nc.vector.tensor_copy(d_plane[:].rearrange("p t m -> p m t"), d_table_scales[:].indirect(ci_list[:]))
+        nc.vector.tensor_copy(d_codes[:].rearrange("p t m -> p m t"), d_table[:].indirect(ci_list[:]))
+        nc.vector.tensor_copy(x_plane[:], x_table_scales[:].indirect(offs_list[:]))
+        nc.vector.tensor_copy(x_codes[:], x_table[:].indirect(offs_list[:]))
+
+        st_rows = []
+        for t in range(PACK):
+            s_bank = psum.tile([P, S], F32, name=f"s_bank{t}")
+            nc.tensor.matmul_mx(
+                out=s_bank[:],
+                lhsT=d_codes[:, t, :].bitcast(FP8X4),
+                lhsT_scale=d_plane[:, t, :],
+                rhs=x_codes[:].bitcast(FP8X4),
+                rhs_scale=x_plane[:],
+                start=True,
+                stop=True,
+            )
+            nc.vector.tensor_scalar(s_rows[t][:, :S], s_bank[:], SCORE_SCALE, None, ALU.mult)
+
+        nc.vector.scalar_tensor_tensor(bias[:], slope[:], -1.0, threshold[:], ALU.mult, ALU.mult)
+
+        gained = keep.tile([P, PACK, S], F32, name="gained")
+        for t in range(PACK):
+            s_at_n1 = keep.tile([P, S], F32, name=f"s_at_n1_{t}")
+            nc.scalar.activation(s_at_n1[:], s_rows[t][:].indirect(n1_list[:]), ACT.Copy)
+            st_row = keep.tile([P, S], F32, name=f"st_row{t}")
+            nc.vector.tensor_tensor(st_row[:], s_rows[t][:, :S], s_at_n1[:], ALU.max)
+            nc.vector.tensor_scalar(gained[:, t, :], st_row[:], gain[:, t : t + 1], None, ALU.mult)
+            st_rows.append(st_row)
+
+        h_banks = [psum.tile([P, S], F32, name=f"h_bank{m}") for m in range(N // P)]
+        rl_rows = [keep.tile([P, S], F32, name=f"rl_row{m}") for m in range(N // P)]
+        ds_rows = [keep.tile([P, S], F32, name=f"ds_row{m}") for m in range(N // P)]
+
+        for a in range(2):
+            cols = slice(a * HALF, (a + 1) * HALF)
+            sg = keep.tile([P, PACK, HALF], F32, name=f"sg{a}")
+            for t in range(PACK):
+                nc.scalar.activation(
+                    sg[:, t, :], st_rows[t][:].indirect(half_of(n2_list, a)), ACT.Sigmoid, bias=bias[:, t : t + 1], scale=slope[:, t : t + 1]
+                )
+            z_packed = keep.tile([P, HALF, PACK], BF16, name="z_packed", align_bytes=64)
+            nc.vector.tensor_tensor(
+                z_packed[:].rearrange("p (c i) t -> p c t i", i=4),
+                gained[:, :, cols].rearrange("p t (c i) -> p c t i", i=4),
+                sg[:].rearrange("p t (c i) -> p c t i", i=4),
+                ALU.mult,
+            )
+            z_codes = keep.tile([P, HALF], U32, name=f"z_codes{a}", align_bytes=64)
+            z_plane = keep.tile([P, HALF], U8, name=f"z_plane{a}", align_bytes=64)
+            nc.vector.quantize_mx(out=z_codes[:].bitcast(FP8X4), scales=z_plane[:], in_=z_packed[:].rearrange("p c t -> p (c t)"))
+            for m in range(N // P):
+                nc.tensor.matmul_mx(
+                    out=h_banks[m][:, cols],
+                    lhsT=w1_codes[:, 2 * P * m : 2 * P * (m + 1)].bitcast(FP4X4),
+                    lhsT_scale=w1_plane[:, P * m : P * (m + 1)],
+                    rhs=z_codes[:].bitcast(FP8X4),
+                    rhs_scale=z_plane[:],
+                    start=True,
+                    stop=True,
+                )
+                if (a, m) == (0, 0):
+                    nc.scalar.activation(rl_rows[m][:, cols], h_banks[m][:, cols], ACT.Relu)
+                else:
+                    nc.vector.tensor_scalar(rl_rows[m][:, cols], h_banks[m][:, cols], 0.0, None, ALU.max)
+
+        for a in range(2):
+            cols = slice(a * HALF, (a + 1) * HALF)
+            for m in range(N // P):
+                nc.scalar.activation(ds_rows[m][:].indirect(half_of(n3_list, a)), rl_rows[m][:, cols], ACT.Copy)
+
+        for m in range(N // P):
+            result = keep.tile([P, S], F32, name=f"result{m}")
+            nc.vector.scalar_tensor_tensor(result[:], h_banks[m][:], -0.5, ds_rows[m][:], ALU.mult, ALU.add)
+            nc.sync.dma_start(out=out[P * m : P * (m + 1), :], in_=result[:])

@@ -72,6 +72,10 @@ def tile_picked_dwlehhsend_none_p_kernel(tc, x_words, x_scales, d_words, d_scale
         load_scale_rows([nc.scalar] * 4, d_table_scales, d_scales)
         nc.sync.dma_start(out=x_table[:].bitcast(I32), in_=x_words[0].rearrange("p n t -> p (n t)").bitcast(I32))
         load_scale_rows([nc.scalar] * 3 + [nc.gpsimd], x_table_scales, x_scales)
+        warm_in = keep.tile([P, 1], F32, name="warm_in")
+        warm_out = keep.tile([P, 1], F32, name="warm_out")
+        nc.vector.memset(warm_in[:], 0.0)
+        nc.scalar.activation(warm_out[:], warm_in[:], ACT.Sigmoid)
         load_scale_rows([nc.scalar] * 4, w1_plane, w1_scales)
         nc.sync.dma_start(n1_list[:], n1)
         nc.sync.dma_start(n2_list[:], n2)

@@ -21,14 +21,17 @@ H = 512
 N = 512
 HALF = S // 2
 LIST_ROWS = 16
+X_PLANE_ROW = 4
+D_PLANE_ROW = 8
+CHUNKS = (slice(0, 64), slice(64, 128), slice(128, 256))
 SCORE_SCALE = 0.0625
 
 FLOPS = 2 * 512 * H * S + 2 * H * N * S
 
 
-def load_scale_rows(queues, plane, scales):
+def load_scale_rows(queues, plane, scales, first_row):
     for q, queue in enumerate(queues):
-        queue.dma_start(out=plane[32 * q : 32 * q + 4, :].bitcast(I32), in_=scales[0, 4 * q : 4 * q + 4, :].bitcast(I32))
+        queue.dma_start(out=plane[32 * q + first_row : 32 * q + first_row + 4, :].bitcast(I32), in_=scales[0, 4 * q : 4 * q + 4, :].bitcast(I32))
 
 
 def tile_picked_dwlehhsend_none_p_kernel(tc, x_words, x_scales, d_words, d_scales, sl, th, gn, w1_words, w1_scales, offs, ci, n1, n2, n3, out):
@@ -37,9 +40,8 @@ def tile_picked_dwlehhsend_none_p_kernel(tc, x_words, x_scales, d_words, d_scale
         keep = ctx.enter_context(tc.tile_pool(name="keep", bufs=1))
         psum = ctx.enter_context(tc.psum_pool(name="psum", bufs=1))
 
-        def half_of(list_tile, a):
-            cols = HALF // LIST_ROWS
-            return list_tile[:, a * cols : (a + 1) * cols]
+        def entries(list_tile, cols):
+            return list_tile[:, cols.start // LIST_ROWS : cols.stop // LIST_ROWS]
 
         ci_list = keep.tile([P, H // LIST_ROWS], U16, name="ci_list")
         offs_list = keep.tile([P, S // LIST_ROWS], U16, name="offs_list")
@@ -66,22 +68,30 @@ def tile_picked_dwlehhsend_none_p_kernel(tc, x_words, x_scales, d_words, d_scale
         for s_row in s_rows:
             nc.vector.memset(s_row[:, S:], 0.0)
 
+        z_codes = [keep.tile([P, P], U32, name=f"z_codes{c}", align_bytes=64) for c in range(len(CHUNKS))]
+        z_planes = [keep.tile([P, P], U8, name=f"z_plane{c}", align_bytes=64) for c in range(len(CHUNKS))]
+        for c, cols in enumerate(CHUNKS):
+            width = cols.stop - cols.start
+            if width < P:
+                nc.vector.memset(z_codes[c][:, width:].bitcast(I32), 0)
+                nc.vector.memset(z_planes[c][:, width:].bitcast(I32), 0)
+
         nc.sync.dma_start(ci_list[:], ci)
         nc.sync.dma_start(offs_list[:], offs)
         nc.sync.dma_start(out=d_table[:].bitcast(I32), in_=d_words[0].rearrange("p n t -> p (n t)").bitcast(I32))
-        load_scale_rows([nc.scalar] * 4, d_table_scales, d_scales)
+        load_scale_rows([nc.scalar] * 4, d_table_scales, d_scales, D_PLANE_ROW)
         nc.sync.dma_start(out=x_table[:].bitcast(I32), in_=x_words[0].rearrange("p n t -> p (n t)").bitcast(I32))
-        load_scale_rows([nc.scalar] * 3 + [nc.gpsimd], x_table_scales, x_scales)
+        load_scale_rows([nc.scalar] * 3 + [nc.gpsimd], x_table_scales, x_scales, X_PLANE_ROW)
         warm_in = keep.tile([P, 1], F32, name="warm_in")
         warm_out = keep.tile([P, 1], F32, name="warm_out")
         nc.vector.memset(warm_in[:], 0.0)
         nc.scalar.activation(warm_out[:], warm_in[:], ACT.Sigmoid)
-        load_scale_rows([nc.scalar] * 4, w1_plane, w1_scales)
+        load_scale_rows([nc.scalar] * 4, w1_plane, w1_scales, 0)
         nc.sync.dma_start(n1_list[:], n1)
-        nc.sync.dma_start(n2_list[:], n2)
+        nc.sync.dma_start(out=gain[:], in_=gn.rearrange("(p t) o -> p (t o)", t=PACK))
         nc.sync.dma_start(out=slope[:], in_=sl.rearrange("(p t) o -> p (t o)", t=PACK))
         nc.sync.dma_start(out=threshold[:], in_=th.rearrange("(p t) o -> p (t o)", t=PACK))
-        nc.sync.dma_start(out=gain[:], in_=gn.rearrange("(p t) o -> p (t o)", t=PACK))
+        nc.sync.dma_start(n2_list[:], n2)
         nc.sync.dma_start(out=w1_codes[:].bitcast(I32), in_=w1_words[0].bitcast(I32))
         nc.sync.dma_start(n3_list[:], n3)
 
@@ -92,22 +102,39 @@ def tile_picked_dwlehhsend_none_p_kernel(tc, x_words, x_scales, d_words, d_scale
         nc.vector.tensor_copy(d_plane[:].rearrange("p t m -> p m t"), d_table_scales[:].indirect(ci_list[:]))
         nc.vector.tensor_copy(d_codes[:].rearrange("p t m -> p m t"), d_table[:].indirect(ci_list[:]))
         nc.vector.tensor_copy(x_plane[:], x_table_scales[:].indirect(offs_list[:]))
-        nc.vector.tensor_copy(x_codes[:], x_table[:].indirect(offs_list[:]))
+        halves = (slice(0, HALF), slice(HALF, S))
+        for cols in halves:
+            nc.vector.tensor_copy(x_codes[:, cols], x_table[:].indirect(entries(offs_list, cols)))
 
-        st_rows = []
-        for t in range(PACK):
-            s_bank = psum.tile([P, S], F32, name=f"s_bank{t}")
+        def score(t, cols, bank):
             nc.tensor.matmul_mx(
-                out=s_bank[:],
+                out=bank,
                 lhsT=d_codes[:, t, :].bitcast(FP8X4),
-                lhsT_scale=d_plane[:, t, :],
-                rhs=x_codes[:].bitcast(FP8X4),
-                rhs_scale=x_plane[:],
+                lhsT_scale=d_plane[D_PLANE_ROW:, t, :],
+                rhs=x_codes[:, cols].bitcast(FP8X4),
+                rhs_scale=x_plane[X_PLANE_ROW:, cols],
                 start=True,
                 stop=True,
             )
-            nc.vector.tensor_scalar(s_rows[t][:, :S], s_bank[:], SCORE_SCALE, None, ALU.mult)
 
+        def scale_out(t, cols, bank):
+            nc.vector.tensor_scalar(s_rows[t][:, cols], bank, SCORE_SCALE, None, ALU.mult)
+
+        whole = slice(0, S)
+        for a, cols in enumerate(halves):
+            half_bank = psum.tile([P, HALF], F32, name=f"half_bank{a}")
+            score(0, cols, half_bank[:])
+            scale_out(0, cols, half_bank[:])
+        second_bank = psum.tile([P, S], F32, name="second_bank")
+        score(1, whole, second_bank[:])
+        scale_out(1, whole, second_bank[:])
+        last_bank = psum.tile([P, 2, S], F32, name="last_bank")
+        for t in (2, 3):
+            score(t, whole, last_bank[:, t - 2, :])
+        for t in (2, 3):
+            scale_out(t, whole, last_bank[:, t - 2, :])
+
+        st_rows = []
         nc.vector.scalar_tensor_tensor(bias[:], slope[:], -1.0, threshold[:], ALU.mult, ALU.mult)
 
         gained = keep.tile([P, PACK, S], F32, name="gained")
@@ -123,44 +150,42 @@ def tile_picked_dwlehhsend_none_p_kernel(tc, x_words, x_scales, d_words, d_scale
         rl_rows = [keep.tile([P, S], F32, name=f"rl_row{m}") for m in range(N // P)]
         ds_rows = [keep.tile([P, S], F32, name=f"ds_row{m}") for m in range(N // P)]
 
-        for a in range(2):
-            cols = slice(a * HALF, (a + 1) * HALF)
-            sg = keep.tile([P, PACK, HALF], F32, name=f"sg{a}")
+        for c, cols in enumerate(CHUNKS):
+            width = cols.stop - cols.start
+            sg = keep.tile([P, PACK, width], F32, name=f"sg{c}")
             for t in range(PACK):
                 nc.scalar.activation(
-                    sg[:, t, :], st_rows[t][:].indirect(half_of(n2_list, a)), ACT.Sigmoid, bias=bias[:, t : t + 1], scale=slope[:, t : t + 1]
+                    sg[:, t, :], st_rows[t][:].indirect(entries(n2_list, cols)), ACT.Sigmoid, bias=bias[:, t : t + 1], scale=slope[:, t : t + 1]
                 )
-            z_packed = keep.tile([P, HALF, PACK], BF16, name="z_packed", align_bytes=64)
+            z_packed = keep.tile([P, width, PACK], BF16, name="z_packed", align_bytes=64)
             nc.vector.tensor_tensor(
                 z_packed[:].rearrange("p (c i) t -> p c t i", i=4),
                 gained[:, :, cols].rearrange("p t (c i) -> p c t i", i=4),
                 sg[:].rearrange("p t (c i) -> p c t i", i=4),
                 ALU.mult,
             )
-            z_codes = keep.tile([P, HALF], U32, name=f"z_codes{a}", align_bytes=64)
-            z_plane = keep.tile([P, HALF], U8, name=f"z_plane{a}", align_bytes=64)
-            nc.vector.quantize_mx(out=z_codes[:].bitcast(FP8X4), scales=z_plane[:], in_=z_packed[:].rearrange("p c t -> p (c t)"))
+            nc.vector.quantize_mx(
+                out=z_codes[c][:, :width].bitcast(FP8X4), scales=z_planes[c][:, :width], in_=z_packed[:].rearrange("p c t -> p (c t)")
+            )
             for m in range(N // P):
                 nc.tensor.matmul_mx(
-                    out=h_banks[m][:, cols],
+                    out=h_banks[m][:, cols.start : cols.start + P],
                     lhsT=w1_codes[:, 2 * P * m : 2 * P * (m + 1)].bitcast(FP4X4),
                     lhsT_scale=w1_plane[:, P * m : P * (m + 1)],
-                    rhs=z_codes[:].bitcast(FP8X4),
-                    rhs_scale=z_plane[:],
+                    rhs=z_codes[c][:].bitcast(FP8X4),
+                    rhs_scale=z_planes[c][:],
                     start=True,
                     stop=True,
                 )
-                if (a, m) == (0, 0):
-                    nc.scalar.activation(rl_rows[m][:, cols], h_banks[m][:, cols], ACT.Relu)
-                else:
-                    nc.vector.tensor_scalar(rl_rows[m][:, cols], h_banks[m][:, cols], 0.0, None, ALU.max)
+                nc.vector.tensor_scalar(rl_rows[m][:, cols], h_banks[m][:, cols], 0.0, None, ALU.max)
 
-        for a in range(2):
-            cols = slice(a * HALF, (a + 1) * HALF)
+        for cols in CHUNKS:
             for m in range(N // P):
-                nc.scalar.activation(ds_rows[m][:].indirect(half_of(n3_list, a)), rl_rows[m][:, cols], ACT.Copy)
+                nc.scalar.activation(ds_rows[m][:].indirect(entries(n3_list, cols)), rl_rows[m][:, cols], ACT.Copy)
 
         for m in range(N // P):
             result = keep.tile([P, S], F32, name=f"result{m}")
-            nc.vector.scalar_tensor_tensor(result[:], h_banks[m][:], -0.5, ds_rows[m][:], ALU.mult, ALU.add)
-            nc.sync.dma_start(out=out[P * m : P * (m + 1), :], in_=result[:])
+            pieces = zip(halves, (nc.sync, nc.scalar)) if m == N // P - 1 else [(whole, nc.sync)]
+            for cols, queue in pieces:
+                nc.vector.scalar_tensor_tensor(result[:, cols], h_banks[m][:, cols], -0.5, ds_rows[m][:, cols], ALU.mult, ALU.add)
+                queue.dma_start(out=out[P * m : P * (m + 1), cols], in_=result[:, cols])

@@ -81,7 +81,7 @@ def tile_picked_dwlehhsend_none_p_kernel(tc, x_words, x_scales, d_words, d_scale
         nc.sync.dma_start(out=d_table[:].bitcast(I32), in_=d_words[0].rearrange("p n t -> p (n t)").bitcast(I32))
         load_scale_rows([nc.scalar] * 4, d_table_scales, d_scales, D_PLANE_ROW)
         nc.sync.dma_start(out=x_table[:].bitcast(I32), in_=x_words[0].rearrange("p n t -> p (n t)").bitcast(I32))
-        load_scale_rows([nc.scalar] * 3 + [nc.gpsimd], x_table_scales, x_scales, X_PLANE_ROW)
+        load_scale_rows([nc.scalar] * 2 + [nc.gpsimd] * 2, x_table_scales, x_scales, X_PLANE_ROW)
         warm_in = keep.tile([P, 1], F32, name="warm_in")
         warm_out = keep.tile([P, 1], F32, name="warm_out")
         nc.vector.memset(warm_in[:], 0.0)

from contextlib import ExitStack

import concourse.mybir as mybir

F32 = mybir.dt.float32
BF16 = mybir.dt.bfloat16
I32 = mybir.dt.int32
U32 = mybir.dt.uint32
U16 = mybir.dt.uint16
U8 = mybir.dt.uint8
FP8X4 = mybir.dt.float8_e4m3fn_x4
FP4X4 = mybir.dt.float4_e2m1fn_x4
ALU = mybir.AluOpType
ACT = mybir.ActivationFunctionType

P = 128
PACK = 4
TABLE = 2048
S = 256
H = 512
N = 512
HALF = S // 2
LIST_ROWS = 16
X_PLANE_ROW = 4
D_PLANE_ROW = 8
CHUNKS = (slice(0, 64), slice(64, 128), slice(128, 256))
SCORE_SCALE = 0.0625

FLOPS = 2 * 512 * H * S + 2 * H * N * S


def load_scale_rows(queues, plane, scales, first_row):
    for q, queue in enumerate(queues):
        queue.dma_start(out=plane[32 * q + first_row : 32 * q + first_row + 4, :].bitcast(I32), in_=scales[0, 4 * q : 4 * q + 4, :].bitcast(I32))


def tile_picked_dwlehhsend_none_p_kernel(tc, x_words, x_scales, d_words, d_scales, sl, th, gn, w1_words, w1_scales, offs, ci, n1, n2, n3, out):
    nc = tc.nc
    with ExitStack() as ctx:
        keep = ctx.enter_context(tc.tile_pool(name="keep", bufs=1))
        psum = ctx.enter_context(tc.psum_pool(name="psum", bufs=1))

        def entries(list_tile, cols):
            return list_tile[:, cols.start // LIST_ROWS : cols.stop // LIST_ROWS]

        ci_list = keep.tile([P, H // LIST_ROWS], U16, name="ci_list")
        offs_list = keep.tile([P, S // LIST_ROWS], U16, name="offs_list")
        n1_list = keep.tile([P, S // LIST_ROWS], U16, name="n1_list")
        n2_list = keep.tile([P, S // LIST_ROWS], U16, name="n2_list")
        n3_list = keep.tile([P, S // LIST_ROWS], U16, name="n3_list")

        d_table = keep.tile([P, TABLE], U32, name="d_table")
        x_table = keep.tile([P, TABLE], U32, name="x_table")
        d_table_scales = keep.tile([P, TABLE], U8, name="d_table_scales")
        x_table_scales = keep.tile([P, TABLE], U8, name="x_table_scales")
        w1_codes = keep.tile([P, 2 * N], U8, name="w1_codes", align_bytes=64)
        w1_plane = keep.tile([P, N], U8, name="w1_plane", align_bytes=64)
        slope = keep.tile([P, PACK], F32, name="slope")
        threshold = keep.tile([P, PACK], F32, name="threshold")
        gain = keep.tile([P, PACK], F32, name="gain")
        bias = keep.tile([P, PACK], F32, name="bias")

        nc.vector.memset(d_table_scales[:].bitcast(I32), 0)
        nc.vector.memset(x_table_scales[:].bitcast(I32), 0)
        nc.vector.memset(w1_plane[:].bitcast(I32), 0)

        s_rows = [keep.tile([P, 2 * S], F32, name=f"s_row{t}") for t in range(PACK)]
        for s_row in s_rows:
            nc.vector.memset(s_row[:, S:], 0.0)

        z_codes = [keep.tile([P, P], U32, name=f"z_codes{c}", align_bytes=64) for c in range(len(CHUNKS))]
        z_planes = [keep.tile([P, P], U8, name=f"z_plane{c}", align_bytes=64) for c in range(len(CHUNKS))]
        for c, cols in enumerate(CHUNKS):
            width = cols.stop - cols.start
            if width < P:
                nc.vector.memset(z_codes[c][:, width:].bitcast(I32), 0)
                nc.vector.memset(z_planes[c][:, width:].bitcast(I32), 0)

        nc.sync.dma_start(ci_list[:], ci)
        nc.sync.dma_start(offs_list[:], offs)
        nc.sync.dma_start(out=d_table[:].bitcast(I32), in_=d_words[0].rearrange("p n t -> p (n t)").bitcast(I32))
        load_scale_rows([nc.scalar] * 4, d_table_scales, d_scales, D_PLANE_ROW)
        nc.sync.dma_start(out=x_table[:].bitcast(I32), in_=x_words[0].rearrange("p n t -> p (n t)").bitcast(I32))
        load_scale_rows([nc.scalar] * 2 + [nc.gpsimd] * 2, x_table_scales, x_scales, X_PLANE_ROW)
        warm_in = keep.tile([P, 1], F32, name="warm_in")
        warm_out = keep.tile([P, 1], F32, name="warm_out")
        nc.vector.memset(warm_in[:], 0.0)
        nc.scalar.activation(warm_out[:], warm_in[:], ACT.Sigmoid)
        load_scale_rows([nc.scalar] * 4, w1_plane, w1_scales, 0)
        nc.sync.dma_start(n1_list[:], n1)
        nc.sync.dma_start(out=gain[:], in_=gn.rearrange("(p t) o -> p (t o)", t=PACK))
        nc.sync.dma_start(out=slope[:], in_=sl.rearrange("(p t) o -> p (t o)", t=PACK))
        nc.sync.dma_start(out=threshold[:], in_=th.rearrange("(p t) o -> p (t o)", t=PACK))
        nc.sync.dma_start(n2_list[:], n2)
        nc.sync.dma_start(out=w1_codes[:].bitcast(I32), in_=w1_words[0].bitcast(I32))
        nc.sync.dma_start(n3_list[:], n3)

        d_codes = keep.tile([P, PACK, P], U32, name="d_codes", align_bytes=64)
        d_plane = keep.tile([P, PACK, P], U8, name="d_plane", align_bytes=64)
        x_codes = keep.tile([P, S], U32, name="x_codes", align_bytes=64)
        x_plane = keep.tile([P, S], U8, name="x_plane", align_bytes=64)
        nc.vector.tensor_copy(d_plane[:].rearrange("p t m -> p m t"), d_table_scales[:].indirect(ci_list[:]))
        nc.vector.tensor_copy(d_codes[:].rearrange("p t m -> p m t"), d_table[:].indirect(ci_list[:]))
        nc.vector.tensor_copy(x_plane[:], x_table_scales[:].indirect(offs_list[:]))
        halves = (slice(0, HALF), slice(HALF, S))
        for cols in halves:
            nc.vector.tensor_copy(x_codes[:, cols], x_table[:].indirect(entries(offs_list, cols)))

        def score(t, cols, bank):
            nc.tensor.matmul_mx(
                out=bank,
                lhsT=d_codes[:, t, :].bitcast(FP8X4),
                lhsT_scale=d_plane[D_PLANE_ROW:, t, :],
                rhs=x_codes[:, cols].bitcast(FP8X4),
                rhs_scale=x_plane[X_PLANE_ROW:, cols],
                start=True,
                stop=True,
            )

        def scale_out(t, cols, bank):
            nc.vector.tensor_scalar(s_rows[t][:, cols], bank, SCORE_SCALE, None, ALU.mult)

        whole = slice(0, S)
        for a, cols in enumerate(halves):
            half_bank = psum.tile([P, HALF], F32, name=f"half_bank{a}")
            score(0, cols, half_bank[:])
            scale_out(0, cols, half_bank[:])
        second_bank = psum.tile([P, S], F32, name="second_bank")
        score(1, whole, second_bank[:])
        scale_out(1, whole, second_bank[:])
        last_bank = psum.tile([P, 2, S], F32, name="last_bank")
        for t in (2, 3):
            score(t, whole, last_bank[:, t - 2, :])
        for t in (2, 3):
            scale_out(t, whole, last_bank[:, t - 2, :])

        st_rows = []
        nc.vector.scalar_tensor_tensor(bias[:], slope[:], -1.0, threshold[:], ALU.mult, ALU.mult)

        gained = keep.tile([P, PACK, S], F32, name="gained")
        for t in range(PACK):
            s_at_n1 = keep.tile([P, S], F32, name=f"s_at_n1_{t}")
            nc.scalar.activation(s_at_n1[:], s_rows[t][:].indirect(n1_list[:]), ACT.Copy)
            st_row = keep.tile([P, S], F32, name=f"st_row{t}")
            nc.vector.tensor_tensor(st_row[:], s_rows[t][:, :S], s_at_n1[:], ALU.max)
            nc.vector.tensor_scalar(gained[:, t, :], st_row[:], gain[:, t : t + 1], None, ALU.mult)
            st_rows.append(st_row)

        h_banks = [psum.tile([P, S], F32, name=f"h_bank{m}") for m in range(N // P)]
        rl_rows = [keep.tile([P, S], F32, name=f"rl_row{m}") for m in range(N // P)]
        ds_rows = [keep.tile([P, S], F32, name=f"ds_row{m}") for m in range(N // P)]

        for c, cols in enumerate(CHUNKS):
            width = cols.stop - cols.start
            sg = keep.tile([P, PACK, width], F32, name=f"sg{c}")
            for t in range(PACK):
                nc.scalar.activation(
                    sg[:, t, :], st_rows[t][:].indirect(entries(n2_list, cols)), ACT.Sigmoid, bias=bias[:, t : t + 1], scale=slope[:, t : t + 1]
                )
            z_packed = keep.tile([P, width, PACK], BF16, name="z_packed", align_bytes=64)
            nc.vector.tensor_tensor(
                z_packed[:].rearrange("p (c i) t -> p c t i", i=4),
                gained[:, :, cols].rearrange("p t (c i) -> p c t i", i=4),
                sg[:].rearrange("p t (c i) -> p c t i", i=4),
                ALU.mult,
            )
            nc.vector.quantize_mx(
                out=z_codes[c][:, :width].bitcast(FP8X4), scales=z_planes[c][:, :width], in_=z_packed[:].rearrange("p c t -> p (c t)")
            )
            for m in range(N // P):
                nc.tensor.matmul_mx(
                    out=h_banks[m][:, cols.start : cols.start + P],
                    lhsT=w1_codes[:, 2 * P * m : 2 * P * (m + 1)].bitcast(FP4X4),
                    lhsT_scale=w1_plane[:, P * m : P * (m + 1)],
                    rhs=z_codes[c][:].bitcast(FP8X4),
                    rhs_scale=z_planes[c][:],
                    start=True,
                    stop=True,
                )
                nc.vector.tensor_scalar(rl_rows[m][:, cols], h_banks[m][:, cols], 0.0, None, ALU.max)

        for cols in CHUNKS:
            for m in range(N // P):
                nc.scalar.activation(ds_rows[m][:].indirect(entries(n3_list, cols)), rl_rows[m][:, cols], ACT.Copy)

        for m in range(N // P):
            result = keep.tile([P, S], F32, name=f"result{m}")
            pieces = zip(halves, (nc.sync, nc.scalar)) if m == N // P - 1 else [(whole, nc.sync)]
            for cols, queue in pieces:
                nc.vector.scalar_tensor_tensor(result[:, cols], h_banks[m][:, cols], -0.5, ds_rows[m][:, cols], ALU.mult, ALU.add)
                queue.dma_start(out=out[P * m : P * (m + 1), cols], in_=result[:, cols])
